import numpy as np
import ml_dtypes


def mxq(x, axis, fmt="e4m3"):
    dtype, down = {"e4m3": (ml_dtypes.float8_e4m3fn, 7), "e5m2": (ml_dtypes.float8_e5m2, 14)}[fmt]
    v = np.moveaxis(np.asarray(x, np.float32).astype(ml_dtypes.bfloat16).astype(np.float64), axis, -1)
    blocks = v.reshape(v.shape[:-1] + (-1, 32))
    amax = np.abs(blocks).max(-1, keepdims=True)
    byte = np.maximum(np.where(amax > 0, np.frexp(amax)[1] - 1 + 127, 0) - down, 1)
    scale = np.exp2(byte - 127.0)
    codes = (blocks / scale).astype(np.float32).astype(dtype).astype(np.float64)
    return np.moveaxis((codes * scale).reshape(v.shape), -1, axis)


WIDE = False


def mx_kscale(k):
    if not WIDE:
        return np.ones(k)
    levels = np.array([10, -10, 5, -5, 0])
    if k % 512:
        return np.exp2(np.random.permutation(np.resize(levels, k // 32))).repeat(32)
    a = np.empty((k // 512, 16))
    for p in range(k // 512):
        a[p, :8] = np.random.permutation(np.resize(levels, 8))
        for g in range(8):
            far = levels[np.abs(levels - a[p, g]) >= 10]
            a[p, g + 8] = far[np.random.randint(len(far))]
    return np.exp2(a.ravel()).repeat(32)


def f64(x):
    return np.asarray(x).astype(np.float64)


def striped(idx):
    return np.tile(idx.reshape(-1, 16).T, (8, 1)).astype(np.uint16)


def unstriped(offs):
    return offs[:16].T.reshape(-1).astype(np.int64)


E2M1 = np.array([0.0, 0.5, 1.0, 1.5, 2.0, 3.0, 4.0, 6.0, -0.0, -0.5, -1.0, -1.5, -2.0, -3.0, -4.0, -6.0])


def pack_weight(w, fmt):
    k, n = w.shape
    w = f64(np.asarray(w, np.float32).astype(ml_dtypes.bfloat16)).reshape(k // 32, 32, n)
    amax = np.abs(w).max(1)
    if fmt == "e4m3":
        byte = np.frexp(amax)[1] - 1 + 127 - 7
    else:
        mant, ex = np.frexp(amax / 6.0)
        byte = np.where(mant > 0.5, ex, ex - 1) + 127
    byte = np.clip(np.where(amax > 0, byte, 1), 1, 254)
    scaled = (w * np.exp2(127.0 - byte)[:, None, :]).reshape(k, n).astype(np.float32)
    by_word = np.ascontiguousarray(scaled.reshape(k // 512, 128, 4, n).transpose(0, 1, 3, 2))
    if fmt == "e4m3":
        words = by_word.astype(ml_dtypes.float8_e4m3fn).view(np.uint8)
    else:
        c = by_word.astype(ml_dtypes.float4_e2m1fn).view(np.uint8) & 0xF
        words = (c[..., 0::2] | (c[..., 1::2] << 4)).reshape(k // 512, 128, 2 * n)
    return np.ascontiguousarray(words), np.ascontiguousarray(byte.astype(np.uint8).reshape(k // 512, 16, n))


def unpack_weight(words, scales, fmt):
    g, _, n = scales.shape
    words = np.ascontiguousarray(words).reshape(g, 128, n, -1)
    if fmt == "e4m3":
        vals = words.view(ml_dtypes.float8_e4m3fn).astype(np.float64)
    else:
        nib = np.empty((g, 128, n, 4), np.uint8)
        nib[..., 0::2] = words & 0xF
        nib[..., 1::2] = words >> 4
        vals = E2M1[nib]
    vals = vals * np.repeat(np.exp2(scales.astype(np.float64) - 127.0), 8, axis=1)[..., None]
    return vals.transpose(0, 1, 3, 2).reshape(g * 512, n)


def relu2(v):
    return np.maximum(v, 0.0) ** 2


K, T, E, C, N = 2560, 768, 12, 128, 128


def by_expert(wq, xq):
    return np.concatenate([wq[e].T @ xq[:, e * C:(e + 1) * C] for e in range(E)], axis=1)


def setup_inputs():
    n = np.random.standard_normal
    s = mx_kscale(K)[:, None]
    first = np.random.permutation(np.repeat(np.arange(E), T // E))
    second = (first + 1 + np.random.permutation(np.repeat(np.arange(E - 1), -(-T // (E - 1)))[:T])) % E
    while np.bincount(second, minlength=E).max() != T // E:
        load = np.bincount(second, minlength=E); hi, lo = int(load.argmax()), int(load.argmin())
        t = np.flatnonzero((second == hi) & (first != lo))[0]; second[t] = lo
    slot_token = np.empty(E * C, np.int64); pos = np.empty((2, T), np.int64); fill = np.zeros(E, np.int64)
    place = np.stack([np.random.permutation(C) for _ in range(E)])
    for r, deal in enumerate((first, second)):
        for t in np.random.permutation(T):
            e = deal[t]; j = e * C + place[e, fill[e]]; fill[e] += 1; slot_token[j] = t; pos[r, t] = j
    g = np.random.uniform(0.2, 0.8, T)
    w = [pack_weight(m, "e2m1") for m in n((E + 1, K, N)) / np.sqrt(K) / s[None]]
    return {
        "xT": (n((K, T)) * s).astype(np.float32),
        "w_words": np.stack([m[0] for m in w]),
        "w_scales": np.stack([m[1] for m in w]),
        "b": (0.3 * n((N, E + 1))).astype(np.float32),
        "gate": np.stack([np.tile(g, (N, 1)), np.tile(1.0 - g, (N, 1))]).astype(np.float32),
        "offs": striped(slot_token),
        "pos1": striped(pos[0]),
        "pos2": striped(pos[1]),
    }


def reference(xT, w_words, w_scales, b, gate, offs, pos1, pos2):
    idx = unstriped(offs)
    w = np.stack([unpack_weight(w_words[e], w_scales[e], "e2m1") for e in range(E + 1)])
    wq = w
    xs = mxq(f64(xT), 0, "e4m3")
    ys = relu2((wq[E].T @ xs) + f64(b)[:, E:])
    xq = mxq(f64(xT)[:, idx], 0, "e4m3")
    y = by_expert(w, xq)
    y = relu2(y + np.repeat(f64(b)[:, :E], C, axis=1))
    return ys + f64(gate[0]) * y[:, unstriped(pos1)] + f64(gate[1]) * y[:, unstriped(pos2)]

@@ -1,0 +1,224 @@
+from contextlib import ExitStack
+
+import concourse.mybir as mybir
+
+K, T, E, C, N = 2560, 768, 12, 128, 128
+S = E * C
+P = 128
+PASSES = K // 512
+FLOPS = 2 * K * N * (S + T)
+
+F32 = mybir.dt.float32
+BF16 = mybir.dt.bfloat16
+U32 = mybir.dt.uint32
+I32 = mybir.dt.int32
+U16 = mybir.dt.uint16
+U8 = mybir.dt.uint8
+FP8 = mybir.dt.float8_e4m3fn_x4
+FP4 = mybir.dt.float4_e2m1fn_x4
+ADD, MULT, MAX = mybir.AluOpType.add, mybir.AluOpType.mult, mybir.AluOpType.max
+RELU = mybir.ActivationFunctionType.Relu
+SQUARE = mybir.ActivationFunctionType.Square
+
+
+def tile_moe_shr_lin_relu2_kernel(tc, xT, w_words, w_scales, b, gate, offs, pos1, pos2, out):
+    nc = tc.nc
+    with ExitStack() as ctx:
+        keep = ctx.enter_context(tc.tile_pool(name="keep", bufs=1))
+        xpool = ctx.enter_context(tc.tile_pool(name="xpool", bufs=8))
+        winp = ctx.enter_context(tc.tile_pool(name="winp", bufs=3))
+        gp = ctx.enter_context(tc.tile_pool(name="gp", bufs=4))
+        gip = ctx.enter_context(tc.tile_pool(name="gip", bufs=3))
+        shp = ctx.enter_context(tc.tile_pool(name="shp", bufs=2))
+        psum = ctx.enter_context(tc.psum_pool(name="psum", bufs=1))
+
+        offs_t = keep.tile([P, S // 16], U16, name="offs_t")
+        pos1_t = keep.tile([P, T // 16], U16, name="pos1_t")
+        pos2_t = keep.tile([P, T // 16], U16, name="pos2_t")
+        bias = keep.tile([P, E + 1], F32, name="bias")
+        gate_t = keep.tile([P, 2, T], F32, name="gate_t")
+        wt = keep.tile([P, (E + 1) * PASSES, 2 * N], U8, name="wt", align_bytes=64)
+        wsc = keep.tile([P, (E + 1) * PASSES, N], U8, name="wsc", align_bytes=64)
+
+        nc.gpsimd.memset(wsc[:].rearrange("p a n -> p (a n)").bitcast(I32), 0)
+
+        xv = xT.rearrange("(a p j) t -> a p j t", a=PASSES, j=4)
+        xr = {}
+        H = T // 2
+
+        def load_x(a, u):
+            t = xpool.tile([P, 2, T], F32, name="xr")
+            if a == 0 and u == 0:
+                nc.sync.dma_start(out=t[:, :, :H], in_=xv[a][:, 2 * u:2 * u + 2, :H])
+                nc.sync.dma_start(out=t[:, :, H:], in_=xv[a][:, 2 * u:2 * u + 2, H:])
+            else:
+                nc.sync.dma_start(out=t[:], in_=xv[a][:, 2 * u:2 * u + 2, :])
+            xr[a, u] = t
+
+        nc.sync.dma_start(offs_t[:], offs)
+        load_x(0, 0)
+        load_x(0, 1)
+        for a in range(1, 4):
+            load_x(a, 0)
+            load_x(a, 1)
+
+        def late_loads():
+            load_x(4, 0)
+            load_x(4, 1)
+            nc.sync.dma_start(out=bias[:], in_=b)
+            wsv = w_scales.bitcast(I32).rearrange("e a q n -> q (e a) n")
+            for q in range(4):
+                nc.sync.dma_start(out=wsc[32 * q:32 * q + 4].rearrange("p a n -> p (a n)").bitcast(I32).rearrange("p (a n) -> p a n", n=N // 4),
+                                  in_=wsv[4 * q:4 * q + 4])
+            wv = w_words.bitcast(I32).rearrange("e a p n -> p (e a) n")
+            wd = wt[:].rearrange("p a n -> p (a n)").bitcast(I32).rearrange("p (a n) -> p a n", n=N // 2)
+            for lo, hi in ((60, 65), (0, 20), (20, 40), (40, 60)):
+                nc.sync.dma_start(out=wd[:, lo:hi, :], in_=wv[:, lo:hi, :])
+            nc.sync.dma_start(out=gate_t[:], in_=gate.rearrange("g p t -> p g t"))
+            nc.sync.dma_start(pos1_t[:], pos1)
+            nc.sync.dma_start(pos2_t[:], pos2)
+
+        win = {}
+        gt = {}
+        gi = {}
+        sh = {}
+        codes, cscale, scodes, sscale = {}, {}, {}, {}
+
+        def cast(a, u):
+            if u == 0:
+                win[a] = winp.tile([P, 2, 2 * T], BF16, name="win", align_bytes=64)
+            d = win[a][:, u, :].rearrange("p (t j) -> p t j", j=2)
+            s = xr[a, u][:].rearrange("p j t -> p t j")
+            if a == 0 and u == 0:
+                nc.vector.tensor_copy(out=d[:, :H, :], in_=s[:, :H, :])
+                nc.scalar.copy(out=d[:, H:, :], in_=s[:, H:, :])
+            else:
+                nc.scalar.copy(out=d, in_=s)
+
+        def gather(a, lo, n):
+            g = gp.tile([P, 2, 512], U32, name="g")
+            for u in range(2):
+                nc.vector.tensor_copy(g[:, u, :n], win[a][:, u, :].bitcast(U32).indirect(offs_t[:, lo // 16:(lo + n) // 16]))
+            gt[a, lo] = g
+
+        def inter(a, lo, n):
+            t = gip.tile([P, 2 * 1024], BF16, name="gi", align_bytes=64)
+            nc.scalar.copy(out=t[:].bitcast(U32)[:, :2 * n].rearrange("p (s u) -> p s u", u=2),
+                           in_=gt[a, lo][:, :, :n].rearrange("p u s -> p s u"))
+            gi[a, lo] = t
+
+        def quant(a, lo, n):
+            if lo == 0:
+                codes[a] = keep.tile([P, S], U32, name="codes%d" % a, align_bytes=64)
+                cscale[a] = keep.tile([P, S], U8, name="cscale%d" % a, align_bytes=64)
+            nc.vector.quantize_mx(out=codes[a][:, lo:lo + n].bitcast(FP8), scales=cscale[a][:, lo:lo + n], in_=gi[a, lo][:, :4 * n])
+
+        def sh_inter(a):
+            t = shp.tile([P, 4 * T], BF16, name="sh", align_bytes=64)
+            nc.scalar.copy(out=t[:].bitcast(U32).rearrange("p (s u) -> p s u", u=2),
+                           in_=win[a][:].rearrange("p u t -> p (u t)").bitcast(U32).rearrange("p (u s) -> p s u", u=2))
+            sh[a] = t
+
+        def sh_quant(a):
+            scodes[a] = keep.tile([P, T], U32, name="scodes%d" % a, align_bytes=64)
+            sscale[a] = keep.tile([P, T], U8, name="sscale%d" % a, align_bytes=64)
+            for lo, n in ((0, 512), (512, 256)):
+                nc.vector.quantize_mx(out=scodes[a][:, lo:lo + n].bitcast(FP8), scales=sscale[a][:, lo:lo + n],
+                                      in_=sh[a][:, 4 * lo:4 * (lo + n)])
+
+        def mm(dst, e, a, cd, cs, cols, start, stop):
+            nc.tensor.matmul_mx(out=dst, lhsT=wt[:, e * PASSES + a, :].bitcast(FP4), lhsT_scale=wsc[:, e * PASSES + a, :],
+                                rhs=cd[:, cols].bitcast(FP8), rhs_scale=cs[:, cols], start=start, stop=stop)
+
+        y = keep.tile([P, S], F32, name="y")
+        r = keep.tile([P, S], F32, name="r")
+        ys = keep.tile([P, T], F32, name="ys")
+        rs = keep.tile([P, T], F32, name="rs")
+
+        ps_s0 = psum.tile([P, 512], F32, name="ps_s0")
+        ps_s1 = psum.tile([P, 256], F32, name="ps_s1")
+        ps_q = [psum.tile([P, 512], F32, name="ps_q%d" % i) for i in range(2)]
+        ps_l = [psum.tile([P, 128], F32, name="ps_l%d" % i) for i in range(4)]
+
+        def shared_mm():
+            for dst, lo, n in ((ps_s0[:], 0, 512), (ps_s1[:, :128], 512, 128), (ps_s1[:, 128:], 640, 128)):
+                for a in range(PASSES):
+                    mm(dst, E, a, scodes[a], sscale[a], slice(lo, lo + n), a == 0, a == PASSES - 1)
+
+        def quad_mm(i):
+            for e in range(4 * i, 4 * i + 4):
+                for a in range(PASSES):
+                    mm(ps_q[i][:, (e % 4) * C:(e % 4 + 1) * C], e, a, codes[a], cscale[a], slice(e * C, (e + 1) * C), a == 0, a == PASSES - 1)
+
+        def quad_out(i):
+            for e in range(4 * i, 4 * i + 4):
+                nc.scalar.activation(out=r[:, e * C:(e + 1) * C], in_=ps_q[i][:, (e % 4) * C:(e % 4 + 1) * C], func=RELU, bias=bias[:, e:e + 1])
+            nc.scalar.activation(out=y[:, 512 * i:512 * i + 512], in_=r[:, 512 * i:512 * i + 512], func=SQUARE)
+
+        def last_mm(e, passes):
+            for a in passes:
+                mm(ps_l[e - 8][:], e, a, codes[a], cscale[a], slice(e * C, (e + 1) * C), a == 0, a == PASSES - 1)
+
+        CH = ((0, 512), (512, 512), (1024, 512))
+        CHL = ((0, 512), (512, 512), (1024, 256), (1280, 256))
+
+        cast(0, 0)
+        cast(0, 1)
+        pend = []
+
+        def flush(depth):
+            while len(pend) > depth:
+                pend.pop(0)()
+
+        for a in range(PASSES):
+            last = a == PASSES - 1
+            if a == 0:
+                late_loads()
+            for i, (lo, n) in enumerate(CHL if last else CH):
+                gather(a, lo, n)
+                inter(a, lo, n)
+                pend.append(lambda a=a, lo=lo, n=n: quant(a, lo, n))
+                if last and i == 0:
+                    flush(1)
+                    for e in range(8, 12):
+                        last_mm(e, range(PASSES - 1))
+                if last and i == 2:
+                    flush(1)
+                    shared_mm()
+                    quad_mm(0)
+                    quad_out(0)
+                if i == 0:
+                    sh_inter(a)
+                    flush(1)
+                    pend.append(lambda a=a: sh_quant(a))
+                if not last and i < 2:
+                    cast(a + 1, i)
+                flush(1)
+        flush(0)
+        quad_mm(1)
+        for e in range(8, 12):
+            last_mm(e, [PASSES - 1])
+        quad_out(1)
+        for e in range(8, 10):
+            nc.scalar.activation(out=r[:, e * C:(e + 1) * C], in_=ps_l[e - 8][:], func=RELU, bias=bias[:, e:e + 1])
+        nc.scalar.activation(out=y[:, 1024:1280], in_=r[:, 1024:1280], func=SQUARE)
+        for e in range(10, 12):
+            nc.scalar.activation(out=r[:, e * C:(e + 1) * C], in_=ps_l[e - 8][:], func=RELU, bias=bias[:, e:e + 1])
+        nc.scalar.activation(out=y[:, 1280:1536], in_=r[:, 1280:1536], func=SQUARE)
+
+        for ps, lo, n in ((ps_s0, 0, 512), (ps_s1, 512, 256)):
+            nc.vector.tensor_scalar(out=rs[:, lo:lo + n], in0=ps[:], scalar1=bias[:, E:E + 1], scalar2=0.0, op0=ADD, op1=MAX)
+        nc.vector.tensor_tensor(ys[:], rs[:], rs[:], MULT)
+
+        g1 = keep.tile([P, T], F32, name="g1")
+        g2 = keep.tile([P, T], F32, name="g2")
+        s1 = keep.tile([P, T], F32, name="s1")
+        ot = keep.tile([P, T], F32, name="ot")
+        for lo, n in ((0, 384), (384, 384)):
+            q = slice(lo // 16, (lo + n) // 16)
+            c = slice(lo, lo + n)
+            nc.vector.tensor_tensor(g1[:, c], y[:].indirect(pos1_t[:, q]), gate_t[:, 0, c], MULT)
+            nc.vector.tensor_tensor(g2[:, c], y[:].indirect(pos2_t[:, q]), gate_t[:, 1, c], MULT)
+            nc.vector.tensor_tensor(s1[:, c], g1[:, c], ys[:, c], ADD)
+            nc.vector.tensor_tensor(ot[:, c], s1[:, c], g2[:, c], ADD)
+            nc.sync.dma_start(out=out[:, c], in_=ot[:, c])

@@ -18,6 +18,7 @@ FP8 = mybir.dt.float8_e4m3fn_x4
 FP4 = mybir.dt.float4_e2m1fn_x4
 ADD, MULT, MAX = mybir.AluOpType.add, mybir.AluOpType.mult, mybir.AluOpType.max
 RELU = mybir.ActivationFunctionType.Relu
+COPY = mybir.ActivationFunctionType.Copy
 SQUARE = mybir.ActivationFunctionType.Square
 
 
@@ -29,6 +30,7 @@ def tile_moe_shr_lin_relu2_kernel(tc, xT, w_words, w_scales, b, gate, offs, pos1
         winp = ctx.enter_context(tc.tile_pool(name="winp", bufs=3))
         gp = ctx.enter_context(tc.tile_pool(name="gp", bufs=4))
         gip = ctx.enter_context(tc.tile_pool(name="gip", bufs=3))
+        gsp = ctx.enter_context(tc.tile_pool(name="gsp", bufs=2))
         shp = ctx.enter_context(tc.tile_pool(name="shp", bufs=2))
         psum = ctx.enter_context(tc.psum_pool(name="psum", bufs=1))
 
@@ -91,20 +93,39 @@ def tile_moe_shr_lin_relu2_kernel(tc, xT, w_words, w_scales, b, gate, offs, pos1
             s = xr[a, u][:].rearrange("p j t -> p t j")
             if a == 0 and u == 0:
                 nc.vector.tensor_copy(out=d[:, :H, :], in_=s[:, :H, :])
-                nc.scalar.copy(out=d[:, H:, :], in_=s[:, H:, :])
+                nc.vector.tensor_copy(out=d[:, H:, :], in_=s[:, H:, :])
             else:
                 nc.scalar.copy(out=d, in_=s)
 
+        planes = keep.tile([P, 2, T], BF16, name="planes")
+
+        def s_cast():
+            nc.scalar.copy(out=planes[:], in_=xr[4, 1][:])
+
+        def s_gather(lo, n):
+            base = lo // 512 * 512
+            if (4, base) not in gt:
+                gt[4, base] = gsp.tile([P, 2, 512], U32, name="gs")
+            v = gt[4, base][:, 1, :].bitcast(BF16).rearrange("p (s j) -> p s j", j=2)
+            for s0 in range(lo - base, lo - base + n, C):
+                for j in range(2):
+                    nc.scalar.activation(v[:, s0:s0 + C, j], planes[:, j, :].indirect(offs_t[:, (base + s0) // 16:(base + s0 + C) // 16]), COPY)
+
         def gather(a, lo, n):
-            g = gp.tile([P, 2, 512], U32, name="g")
-            for u in range(2):
+            scal = (a, lo) in gt
+            g = gt[a, lo] if scal else gp.tile([P, 2, 512], U32, name="g")
+            for u in range(1 if scal else 2):
                 nc.vector.tensor_copy(g[:, u, :n], win[a][:, u, :].bitcast(U32).indirect(offs_t[:, lo // 16:(lo + n) // 16]))
             gt[a, lo] = g
 
         def inter(a, lo, n):
             t = gip.tile([P, 2 * 1024], BF16, name="gi", align_bytes=64)
-            nc.scalar.copy(out=t[:].bitcast(U32)[:, :2 * n].rearrange("p (s u) -> p s u", u=2),
-                           in_=gt[a, lo][:, :, :n].rearrange("p u s -> p s u"))
+            if (a, lo) == (4, 1280):
+                nc.vector.tensor_copy(out=t[:].bitcast(I32)[:, :2 * n].rearrange("p (s u) -> p s u", u=2),
+                                      in_=gt[a, lo][:, :, :n].bitcast(I32).rearrange("p u s -> p s u"))
+            else:
+                nc.scalar.copy(out=t[:].bitcast(U32)[:, :2 * n].rearrange("p (s u) -> p s u", u=2),
+                               in_=gt[a, lo][:, :, :n].rearrange("p u s -> p s u"))
             gi[a, lo] = t
 
         def quant(a, lo, n):
@@ -131,9 +152,9 @@ def tile_moe_shr_lin_relu2_kernel(tc, xT, w_words, w_scales, b, gate, offs, pos1
                                 rhs=cd[:, cols].bitcast(FP8), rhs_scale=cs[:, cols], start=start, stop=stop)
 
         y = keep.tile([P, S], F32, name="y")
-        r = keep.tile([P, S], F32, name="r")
+        r = y
         ys = keep.tile([P, T], F32, name="ys")
-        rs = keep.tile([P, T], F32, name="rs")
+        rs = ys
 
         ps_s0 = psum.tile([P, 512], F32, name="ps_s0")
         ps_s1 = psum.tile([P, 256], F32, name="ps_s1")
@@ -162,57 +183,81 @@ def tile_moe_shr_lin_relu2_kernel(tc, xT, w_words, w_scales, b, gate, offs, pos1
         CH = ((0, 512), (512, 512), (1024, 512))
         CHL = ((0, 512), (512, 512), (1024, 256), (1280, 256))
 
+        def last_relu(e, vector):
+            cols = slice(e * C, (e + 1) * C)
+            if vector:
+                nc.vector.tensor_scalar(out=r[:, cols], in0=ps_l[e - 8][:], scalar1=bias[:, e:e + 1], scalar2=0.0, op0=ADD, op1=MAX)
+            else:
+                nc.scalar.activation(out=r[:, cols], in_=ps_l[e - 8][:], func=RELU, bias=bias[:, e:e + 1])
+
         cast(0, 0)
         cast(0, 1)
+        late_loads()
         pend = []
 
         def flush(depth):
             while len(pend) > depth:
                 pend.pop(0)()
 
-        for a in range(PASSES):
-            last = a == PASSES - 1
-            if a == 0:
-                late_loads()
-            for i, (lo, n) in enumerate(CHL if last else CH):
+        EXTRA = {
+            (1, 1): s_cast,
+            (1, 2): lambda: s_gather(0, 256),
+            (2, 1): lambda: s_gather(256, 256),
+            (2, 2): lambda: s_gather(512, 256),
+            (3, 1): lambda: s_gather(768, 256),
+        }
+        for a in range(PASSES - 1):
+            for i, (lo, n) in enumerate(CH):
                 gather(a, lo, n)
                 inter(a, lo, n)
                 pend.append(lambda a=a, lo=lo, n=n: quant(a, lo, n))
-                if last and i == 0:
-                    flush(1)
-                    for e in range(8, 12):
-                        last_mm(e, range(PASSES - 1))
-                if last and i == 2:
-                    flush(1)
-                    shared_mm()
-                    quad_mm(0)
-                    quad_out(0)
+                flush(1)
                 if i == 0:
                     sh_inter(a)
-                    flush(1)
                     pend.append(lambda a=a: sh_quant(a))
-                if not last and i < 2:
+                if (a, i) in EXTRA:
+                    EXTRA[a, i]()
+                if i < 2:
                     cast(a + 1, i)
-                flush(1)
+                elif a == PASSES - 2:
+                    sh_inter(a + 1)
+                    pend.append(lambda a=a: sh_quant(a + 1))
+        a = PASSES - 1
+        for i, (lo, n) in enumerate(CHL):
+            gather(a, lo, n)
+            inter(a, lo, n)
+            pend.append(lambda lo=lo, n=n: quant(a, lo, n))
+            flush(1)
+            if i == 0:
+                for e in range(8, 12):
+                    last_mm(e, range(PASSES - 1))
+                shared_mm()
+            elif i == 1:
+                quad_mm(0)
+                quad_out(0)
+            elif i == 2:
+                quad_mm(1)
+            else:
+                quad_out(1)
+                last_mm(8, [a])
+                last_mm(9, [a])
         flush(0)
-        quad_mm(1)
-        for e in range(8, 12):
-            last_mm(e, [PASSES - 1])
-        quad_out(1)
-        for e in range(8, 10):
-            nc.scalar.activation(out=r[:, e * C:(e + 1) * C], in_=ps_l[e - 8][:], func=RELU, bias=bias[:, e:e + 1])
+        last_mm(10, [a])
+        last_mm(11, [a])
+        last_relu(8, False)
+        last_relu(9, False)
         nc.scalar.activation(out=y[:, 1024:1280], in_=r[:, 1024:1280], func=SQUARE)
-        for e in range(10, 12):
-            nc.scalar.activation(out=r[:, e * C:(e + 1) * C], in_=ps_l[e - 8][:], func=RELU, bias=bias[:, e:e + 1])
-        nc.scalar.activation(out=y[:, 1280:1536], in_=r[:, 1280:1536], func=SQUARE)
+        last_relu(10, True)
+        last_relu(11, True)
+        nc.vector.tensor_tensor(y[:, 1280:1536], r[:, 1280:1536], r[:, 1280:1536], MULT)
 
         for ps, lo, n in ((ps_s0, 0, 512), (ps_s1, 512, 256)):
             nc.vector.tensor_scalar(out=rs[:, lo:lo + n], in0=ps[:], scalar1=bias[:, E:E + 1], scalar2=0.0, op0=ADD, op1=MAX)
-        nc.vector.tensor_tensor(ys[:], rs[:], rs[:], MULT)
+            nc.vector.tensor_tensor(ys[:, lo:lo + n], rs[:, lo:lo + n], rs[:, lo:lo + n], MULT)
 
         g1 = keep.tile([P, T], F32, name="g1")
         g2 = keep.tile([P, T], F32, name="g2")
-        s1 = keep.tile([P, T], F32, name="s1")
+        s1 = g1
         ot = keep.tile([P, T], F32, name="ot")
         for lo, n in ((0, 384), (384, 384)):
             q = slice(lo // 16, (lo + n) // 16)

@@ -6,6 +6,7 @@ K, T, E, C, N = 2560, 768, 12, 128, 128
 S = E * C
 P = 128
 PASSES = K // 512
+VINTER = {(4, 1280)}
 FLOPS = 2 * K * N * (S + T)
 
 F32 = mybir.dt.float32
@@ -17,8 +18,8 @@ U8 = mybir.dt.uint8
 FP8 = mybir.dt.float8_e4m3fn_x4
 FP4 = mybir.dt.float4_e2m1fn_x4
 ADD, MULT, MAX = mybir.AluOpType.add, mybir.AluOpType.mult, mybir.AluOpType.max
-RELU = mybir.ActivationFunctionType.Relu
 COPY = mybir.ActivationFunctionType.Copy
+RELU = mybir.ActivationFunctionType.Relu
 SQUARE = mybir.ActivationFunctionType.Square
 
 
@@ -27,10 +28,10 @@ def tile_moe_shr_lin_relu2_kernel(tc, xT, w_words, w_scales, b, gate, offs, pos1
     with ExitStack() as ctx:
         keep = ctx.enter_context(tc.tile_pool(name="keep", bufs=1))
         xpool = ctx.enter_context(tc.tile_pool(name="xpool", bufs=8))
-        winp = ctx.enter_context(tc.tile_pool(name="winp", bufs=3))
+        winp = ctx.enter_context(tc.tile_pool(name="winp", bufs=4))
         gp = ctx.enter_context(tc.tile_pool(name="gp", bufs=4))
-        gip = ctx.enter_context(tc.tile_pool(name="gip", bufs=3))
         gsp = ctx.enter_context(tc.tile_pool(name="gsp", bufs=2))
+        gip = ctx.enter_context(tc.tile_pool(name="gip", bufs=4))
         shp = ctx.enter_context(tc.tile_pool(name="shp", bufs=2))
         psum = ctx.enter_context(tc.psum_pool(name="psum", bufs=1))
 
@@ -41,6 +42,21 @@ def tile_moe_shr_lin_relu2_kernel(tc, xT, w_words, w_scales, b, gate, offs, pos1
         gate_t = keep.tile([P, 2, T], F32, name="gate_t")
         wt = keep.tile([P, (E + 1) * PASSES, 2 * N], U8, name="wt", align_bytes=64)
         wsc = keep.tile([P, (E + 1) * PASSES, N], U8, name="wsc", align_bytes=64)
+        planes = keep.tile([P, 2, T], BF16, name="planes")
+        codes = [keep.tile([P, S], U32, name="codes%d" % a, align_bytes=64) for a in range(PASSES)]
+        cscale = [keep.tile([P, S], U8, name="cscale%d" % a, align_bytes=64) for a in range(PASSES)]
+        scodes = [keep.tile([P, T], U32, name="scodes%d" % a, align_bytes=64) for a in range(PASSES)]
+        sscale = [keep.tile([P, T], U8, name="sscale%d" % a, align_bytes=64) for a in range(PASSES)]
+        y = keep.tile([P, S], F32, name="y")
+        ys = keep.tile([P, T], F32, name="ys")
+        g1 = keep.tile([P, T], F32, name="g1")
+        g2 = keep.tile([P, T], F32, name="g2")
+        ot = keep.tile([P, T], F32, name="ot")
+
+        ps_sa = psum.tile([P, 512], F32, name="ps_sa")
+        ps_sb = psum.tile([P, 512], F32, name="ps_sb")
+        ps_q = [psum.tile([P, 512], F32, name="ps_q%d" % i) for i in range(2)]
+        ps_l = [psum.tile([P, 128], F32, name="ps_l%d" % i) for i in range(4)]
 
         nc.gpsimd.memset(wsc[:].rearrange("p a n -> p (a n)").bitcast(I32), 0)
 
@@ -57,13 +73,6 @@ def tile_moe_shr_lin_relu2_kernel(tc, xT, w_words, w_scales, b, gate, offs, pos1
                 nc.sync.dma_start(out=t[:], in_=xv[a][:, 2 * u:2 * u + 2, :])
             xr[a, u] = t
 
-        nc.sync.dma_start(offs_t[:], offs)
-        load_x(0, 0)
-        load_x(0, 1)
-        for a in range(1, 4):
-            load_x(a, 0)
-            load_x(a, 1)
-
         def late_loads():
             load_x(4, 0)
             load_x(4, 1)
@@ -74,64 +83,55 @@ def tile_moe_shr_lin_relu2_kernel(tc, xT, w_words, w_scales, b, gate, offs, pos1
                                   in_=wsv[4 * q:4 * q + 4])
             wv = w_words.bitcast(I32).rearrange("e a p n -> p (e a) n")
             wd = wt[:].rearrange("p a n -> p (a n)").bitcast(I32).rearrange("p (a n) -> p a n", n=N // 2)
-            for lo, hi in ((60, 65), (0, 20), (20, 40), (40, 60)):
+            for lo, hi in ((40, 65), (0, 20), (20, 40)):
                 nc.sync.dma_start(out=wd[:, lo:hi, :], in_=wv[:, lo:hi, :])
             nc.sync.dma_start(out=gate_t[:], in_=gate.rearrange("g p t -> p g t"))
             nc.sync.dma_start(pos1_t[:], pos1)
             nc.sync.dma_start(pos2_t[:], pos2)
 
-        win = {}
-        gt = {}
-        gi = {}
-        sh = {}
-        codes, cscale, scodes, sscale = {}, {}, {}, {}
+        win, gt, goff, gi, sh = {}, {}, {}, {}, {}
 
         def cast(a, u):
-            if u == 0:
+            if a not in win:
                 win[a] = winp.tile([P, 2, 2 * T], BF16, name="win", align_bytes=64)
             d = win[a][:, u, :].rearrange("p (t j) -> p t j", j=2)
             s = xr[a, u][:].rearrange("p j t -> p t j")
             if a == 0 and u == 0:
                 nc.vector.tensor_copy(out=d[:, :H, :], in_=s[:, :H, :])
-                nc.vector.tensor_copy(out=d[:, H:, :], in_=s[:, H:, :])
+                nc.vector.tensor_copy(out=d[:, H:H + 256, :], in_=s[:, H:H + 256, :])
+                nc.scalar.copy(out=d[:, H + 256:, :], in_=s[:, H + 256:, :])
             else:
                 nc.scalar.copy(out=d, in_=s)
-
-        planes = keep.tile([P, 2, T], BF16, name="planes")
 
         def s_cast():
             nc.scalar.copy(out=planes[:], in_=xr[4, 1][:])
 
-        def s_gather(lo, n):
-            base = lo // 512 * 512
-            if (4, base) not in gt:
-                gt[4, base] = gsp.tile([P, 2, 512], U32, name="gs")
-            v = gt[4, base][:, 1, :].bitcast(BF16).rearrange("p (s j) -> p s j", j=2)
-            for s0 in range(lo - base, lo - base + n, C):
+        def s_gather(lo):
+            g = gsp.tile([P, 2, 256], U32, name="gs")
+            gt[4, lo] = g
+            v = g[:, 1, :].bitcast(BF16).rearrange("p (s j) -> p s j", j=2)
+            for s0 in range(0, 256, C):
                 for j in range(2):
-                    nc.scalar.activation(v[:, s0:s0 + C, j], planes[:, j, :].indirect(offs_t[:, (base + s0) // 16:(base + s0 + C) // 16]), COPY)
+                    nc.scalar.activation(v[:, s0:s0 + C, j], planes[:, j, :].indirect(offs_t[:, (lo + s0) // 16:(lo + s0 + C) // 16]), COPY)
 
         def gather(a, lo, n):
-            scal = (a, lo) in gt
-            g = gt[a, lo] if scal else gp.tile([P, 2, 512], U32, name="g")
-            for u in range(1 if scal else 2):
-                nc.vector.tensor_copy(g[:, u, :n], win[a][:, u, :].bitcast(U32).indirect(offs_t[:, lo // 16:(lo + n) // 16]))
-            gt[a, lo] = g
+            us = (0,) if (a, lo) in gt else (0, 1)
+            if (a, lo) not in gt:
+                gt[a, lo] = gp.tile([P, 2, 512], U32, name="g")
+            for u in us:
+                nc.vector.tensor_copy(gt[a, lo][:, u, :n], win[a][:, u, :].bitcast(U32).indirect(offs_t[:, lo // 16:(lo + n) // 16]))
 
         def inter(a, lo, n):
             t = gip.tile([P, 2 * 1024], BF16, name="gi", align_bytes=64)
-            if (a, lo) == (4, 1280):
+            gi[a, lo] = t
+            if (a, lo) in VINTER:
                 nc.vector.tensor_copy(out=t[:].bitcast(I32)[:, :2 * n].rearrange("p (s u) -> p s u", u=2),
                                       in_=gt[a, lo][:, :, :n].bitcast(I32).rearrange("p u s -> p s u"))
             else:
                 nc.scalar.copy(out=t[:].bitcast(U32)[:, :2 * n].rearrange("p (s u) -> p s u", u=2),
                                in_=gt[a, lo][:, :, :n].rearrange("p u s -> p s u"))
-            gi[a, lo] = t
 
         def quant(a, lo, n):
-            if lo == 0:
-                codes[a] = keep.tile([P, S], U32, name="codes%d" % a, align_bytes=64)
-                cscale[a] = keep.tile([P, S], U8, name="cscale%d" % a, align_bytes=64)
             nc.vector.quantize_mx(out=codes[a][:, lo:lo + n].bitcast(FP8), scales=cscale[a][:, lo:lo + n], in_=gi[a, lo][:, :4 * n])
 
         def sh_inter(a):
@@ -141,129 +141,106 @@ def tile_moe_shr_lin_relu2_kernel(tc, xT, w_words, w_scales, b, gate, offs, pos1
             sh[a] = t
 
         def sh_quant(a):
-            scodes[a] = keep.tile([P, T], U32, name="scodes%d" % a, align_bytes=64)
-            sscale[a] = keep.tile([P, T], U8, name="sscale%d" % a, align_bytes=64)
             for lo, n in ((0, 512), (512, 256)):
                 nc.vector.quantize_mx(out=scodes[a][:, lo:lo + n].bitcast(FP8), scales=sscale[a][:, lo:lo + n],
                                       in_=sh[a][:, 4 * lo:4 * (lo + n)])
 
-        def mm(dst, e, a, cd, cs, cols, start, stop):
+        def mm(dst, e, a, cd, cs, cols):
             nc.tensor.matmul_mx(out=dst, lhsT=wt[:, e * PASSES + a, :].bitcast(FP4), lhsT_scale=wsc[:, e * PASSES + a, :],
-                                rhs=cd[:, cols].bitcast(FP8), rhs_scale=cs[:, cols], start=start, stop=stop)
+                                rhs=cd[a][:, cols].bitcast(FP8), rhs_scale=cs[a][:, cols], start=a == 0, stop=a == PASSES - 1)
 
-        y = keep.tile([P, S], F32, name="y")
-        r = y
-        ys = keep.tile([P, T], F32, name="ys")
-        rs = ys
-
-        ps_s0 = psum.tile([P, 512], F32, name="ps_s0")
-        ps_s1 = psum.tile([P, 256], F32, name="ps_s1")
-        ps_q = [psum.tile([P, 512], F32, name="ps_q%d" % i) for i in range(2)]
-        ps_l = [psum.tile([P, 128], F32, name="ps_l%d" % i) for i in range(4)]
-
-        def shared_mm():
-            for dst, lo, n in ((ps_s0[:], 0, 512), (ps_s1[:, :128], 512, 128), (ps_s1[:, 128:], 640, 128)):
-                for a in range(PASSES):
-                    mm(dst, E, a, scodes[a], sscale[a], slice(lo, lo + n), a == 0, a == PASSES - 1)
+        def shared_mm(a):
+            mm(ps_sa[:], E, a, scodes, sscale, slice(0, 512))
+            mm(ps_sb[:], E, a, scodes, sscale, slice(256, 768))
 
         def quad_mm(i):
             for e in range(4 * i, 4 * i + 4):
                 for a in range(PASSES):
-                    mm(ps_q[i][:, (e % 4) * C:(e % 4 + 1) * C], e, a, codes[a], cscale[a], slice(e * C, (e + 1) * C), a == 0, a == PASSES - 1)
+                    mm(ps_q[i][:, (e % 4) * C:(e % 4 + 1) * C], e, a, codes, cscale, slice(e * C, (e + 1) * C))
 
         def quad_out(i):
             for e in range(4 * i, 4 * i + 4):
-                nc.scalar.activation(out=r[:, e * C:(e + 1) * C], in_=ps_q[i][:, (e % 4) * C:(e % 4 + 1) * C], func=RELU, bias=bias[:, e:e + 1])
-            nc.scalar.activation(out=y[:, 512 * i:512 * i + 512], in_=r[:, 512 * i:512 * i + 512], func=SQUARE)
+                nc.scalar.activation(out=y[:, e * C:(e + 1) * C], in_=ps_q[i][:, (e % 4) * C:(e % 4 + 1) * C], func=RELU, bias=bias[:, e:e + 1])
+            nc.scalar.activation(out=y[:, 512 * i:512 * i + 512], in_=y[:, 512 * i:512 * i + 512], func=SQUARE)
 
-        def last_mm(e, passes):
+        def last_mm(es, passes):
             for a in passes:
-                mm(ps_l[e - 8][:], e, a, codes[a], cscale[a], slice(e * C, (e + 1) * C), a == 0, a == PASSES - 1)
+                for e in es:
+                    mm(ps_l[e - 8][:], e, a, codes, cscale, slice(e * C, (e + 1) * C))
 
-        CH = ((0, 512), (512, 512), (1024, 512))
-        CHL = ((0, 512), (512, 512), (1024, 256), (1280, 256))
-
-        def last_relu(e, vector):
-            cols = slice(e * C, (e + 1) * C)
+        def last_out(e0, vector):
+            sq = slice(e0 * C, (e0 + 2) * C)
+            for e in (e0, e0 + 1):
+                cols = slice(e * C, (e + 1) * C)
+                if vector:
+                    nc.vector.tensor_scalar(out=y[:, cols], in0=ps_l[e - 8][:], scalar1=bias[:, e:e + 1], scalar2=0.0, op0=ADD, op1=MAX)
+                else:
+                    nc.scalar.activation(out=y[:, cols], in_=ps_l[e - 8][:], func=RELU, bias=bias[:, e:e + 1])
             if vector:
-                nc.vector.tensor_scalar(out=r[:, cols], in0=ps_l[e - 8][:], scalar1=bias[:, e:e + 1], scalar2=0.0, op0=ADD, op1=MAX)
+                nc.vector.tensor_tensor(y[:, sq], y[:, sq], y[:, sq], MULT)
             else:
-                nc.scalar.activation(out=r[:, cols], in_=ps_l[e - 8][:], func=RELU, bias=bias[:, e:e + 1])
+                nc.scalar.activation(out=y[:, sq], in_=y[:, sq], func=SQUARE)
 
-        cast(0, 0)
-        cast(0, 1)
-        late_loads()
         pend = []
 
         def flush(depth):
             while len(pend) > depth:
                 pend.pop(0)()
 
-        EXTRA = {
-            (1, 1): s_cast,
-            (1, 2): lambda: s_gather(0, 256),
-            (2, 1): lambda: s_gather(256, 256),
-            (2, 2): lambda: s_gather(512, 256),
-            (3, 1): lambda: s_gather(768, 256),
+        def shared(a):
+            sh_inter(a)
+            pend.append(lambda: sh_quant(a))
+
+        nc.sync.dma_start(offs_t[:], offs)
+        for a in range(4):
+            load_x(a, 0)
+            load_x(a, 1)
+        cast(0, 0)
+        cast(0, 1)
+        late_loads()
+
+        L = PASSES - 1
+        steps = [(a, lo, 512) for a in range(3) for lo in (0, 512, 1024)]
+        for lo, n in ((0, 512), (512, 512), (1024, 256), (1280, 256)):
+            steps += [(3, lo, n), (4, lo, n)]
+        hooks = {
+            (0, 0): lambda: (cast(1, 0), cast(1, 1)),
+            (0, 512): lambda: cast(2, 0),
+            (0, 1024): lambda: shared(0),
+            (1, 0): lambda: (last_mm(range(8, 12), [0]), shared(1), s_cast()),
+            (1, 512): lambda: (shared_mm(0), shared_mm(1), s_gather(1024)),
+            (1, 1024): lambda: (cast(2, 1), cast(3, 0)),
+            (2, 0): lambda: (last_mm(range(8, 12), [1]), cast(4, 1)),
+            (2, 512): lambda: cast(4, 0),
+            (2, 1024): lambda: (cast(3, 1), shared(2)),
+            (3, 0): lambda: (last_mm(range(8, 12), [2]), shared_mm(2)),
+            (3, 512): lambda: (quad_mm(0), shared(3), s_gather(1280)),
+            (4, 512): lambda: (shared_mm(3), shared(4), quad_out(0)),
+            (3, 1024): lambda: (quad_mm(1), shared_mm(4)),
+            (4, 1024): lambda: (quad_out(1), last_mm((8, 9), [3])),
+            (3, 1280): lambda: last_mm((8, 9), [4]),
+            (4, 1280): lambda: (last_out(8, False), last_mm((10, 11), [3])),
         }
-        for a in range(PASSES - 1):
-            for i, (lo, n) in enumerate(CH):
-                gather(a, lo, n)
-                inter(a, lo, n)
-                pend.append(lambda a=a, lo=lo, n=n: quant(a, lo, n))
-                flush(1)
-                if i == 0:
-                    sh_inter(a)
-                    pend.append(lambda a=a: sh_quant(a))
-                if (a, i) in EXTRA:
-                    EXTRA[a, i]()
-                if i < 2:
-                    cast(a + 1, i)
-                elif a == PASSES - 2:
-                    sh_inter(a + 1)
-                    pend.append(lambda a=a: sh_quant(a + 1))
-        a = PASSES - 1
-        for i, (lo, n) in enumerate(CHL):
+        for a, lo, n in steps:
             gather(a, lo, n)
             inter(a, lo, n)
-            pend.append(lambda lo=lo, n=n: quant(a, lo, n))
+            pend.append(lambda a=a, lo=lo, n=n: quant(a, lo, n))
             flush(1)
-            if i == 0:
-                for e in range(8, 12):
-                    last_mm(e, range(PASSES - 1))
-                shared_mm()
-            elif i == 1:
-                quad_mm(0)
-                quad_out(0)
-            elif i == 2:
-                quad_mm(1)
-            else:
-                quad_out(1)
-                last_mm(8, [a])
-                last_mm(9, [a])
+            if (a, lo) in hooks:
+                hooks[a, lo]()
         flush(0)
-        last_mm(10, [a])
-        last_mm(11, [a])
-        last_relu(8, False)
-        last_relu(9, False)
-        nc.scalar.activation(out=y[:, 1024:1280], in_=r[:, 1024:1280], func=SQUARE)
-        last_relu(10, True)
-        last_relu(11, True)
-        nc.vector.tensor_tensor(y[:, 1280:1536], r[:, 1280:1536], r[:, 1280:1536], MULT)
+        last_mm((10, 11), [4])
+        last_out(10, True)
 
-        for ps, lo, n in ((ps_s0, 0, 512), (ps_s1, 512, 256)):
-            nc.vector.tensor_scalar(out=rs[:, lo:lo + n], in0=ps[:], scalar1=bias[:, E:E + 1], scalar2=0.0, op0=ADD, op1=MAX)
-            nc.vector.tensor_tensor(ys[:, lo:lo + n], rs[:, lo:lo + n], rs[:, lo:lo + n], MULT)
+        nc.vector.tensor_scalar(out=ys[:, 512:], in0=ps_sb[:, 256:], scalar1=bias[:, E:E + 1], scalar2=0.0, op0=ADD, op1=MAX)
+        nc.vector.tensor_tensor(ys[:, 512:], ys[:, 512:], ys[:, 512:], MULT)
+        nc.scalar.activation(out=ys[:, :512], in_=ps_sa[:], func=RELU, bias=bias[:, E:E + 1])
+        nc.scalar.activation(out=ys[:, :512], in_=ys[:, :512], func=SQUARE)
 
-        g1 = keep.tile([P, T], F32, name="g1")
-        g2 = keep.tile([P, T], F32, name="g2")
-        s1 = g1
-        ot = keep.tile([P, T], F32, name="ot")
-        for lo, n in ((0, 384), (384, 384)):
-            q = slice(lo // 16, (lo + n) // 16)
+        nc.vector.tensor_tensor(g1[:], y[:].indirect(pos1_t[:]), gate_t[:, 0, :], MULT)
+        nc.vector.tensor_tensor(g1[:], g1[:], ys[:], ADD)
+        for lo, n in ((0, 512), (512, 256)):
             c = slice(lo, lo + n)
-            nc.vector.tensor_tensor(g1[:, c], y[:].indirect(pos1_t[:, q]), gate_t[:, 0, c], MULT)
-            nc.vector.tensor_tensor(g2[:, c], y[:].indirect(pos2_t[:, q]), gate_t[:, 1, c], MULT)
-            nc.vector.tensor_tensor(s1[:, c], g1[:, c], ys[:, c], ADD)
-            nc.vector.tensor_tensor(ot[:, c], s1[:, c], g2[:, c], ADD)
+            nc.vector.tensor_tensor(g2[:, c], y[:].indirect(pos2_t[:, lo // 16:(lo + n) // 16]), gate_t[:, 1, c], MULT)
+            nc.vector.tensor_tensor(ot[:, c], g1[:, c], g2[:, c], ADD)
             nc.sync.dma_start(out=out[:, c], in_=ot[:, c])

from contextlib import ExitStack

import concourse.mybir as mybir

K, T, E, C, N = 2560, 768, 12, 128, 128
S = E * C
P = 128
PASSES = K // 512
VINTER = {(4, 1280)}
FLOPS = 2 * K * N * (S + T)

F32 = mybir.dt.float32
BF16 = mybir.dt.bfloat16
U32 = mybir.dt.uint32
I32 = mybir.dt.int32
U16 = mybir.dt.uint16
U8 = mybir.dt.uint8
FP8 = mybir.dt.float8_e4m3fn_x4
FP4 = mybir.dt.float4_e2m1fn_x4
ADD, MULT, MAX = mybir.AluOpType.add, mybir.AluOpType.mult, mybir.AluOpType.max
COPY = mybir.ActivationFunctionType.Copy
RELU = mybir.ActivationFunctionType.Relu
SQUARE = mybir.ActivationFunctionType.Square


def tile_moe_shr_lin_relu2_kernel(tc, xT, w_words, w_scales, b, gate, offs, pos1, pos2, out):
    nc = tc.nc
    with ExitStack() as ctx:
        keep = ctx.enter_context(tc.tile_pool(name="keep", bufs=1))
        xpool = ctx.enter_context(tc.tile_pool(name="xpool", bufs=8))
        winp = ctx.enter_context(tc.tile_pool(name="winp", bufs=4))
        gp = ctx.enter_context(tc.tile_pool(name="gp", bufs=4))
        gsp = ctx.enter_context(tc.tile_pool(name="gsp", bufs=2))
        gip = ctx.enter_context(tc.tile_pool(name="gip", bufs=4))
        shp = ctx.enter_context(tc.tile_pool(name="shp", bufs=2))
        psum = ctx.enter_context(tc.psum_pool(name="psum", bufs=1))

        offs_t = keep.tile([P, S // 16], U16, name="offs_t")
        pos1_t = keep.tile([P, T // 16], U16, name="pos1_t")
        pos2_t = keep.tile([P, T // 16], U16, name="pos2_t")
        bias = keep.tile([P, E + 1], F32, name="bias")
        gate_t = keep.tile([P, 2, T], F32, name="gate_t")
        wt = keep.tile([P, (E + 1) * PASSES, 2 * N], U8, name="wt", align_bytes=64)
        wsc = keep.tile([P, (E + 1) * PASSES, N], U8, name="wsc", align_bytes=64)
        planes = keep.tile([P, 2, T], BF16, name="planes")
        codes = [keep.tile([P, S], U32, name="codes%d" % a, align_bytes=64) for a in range(PASSES)]
        cscale = [keep.tile([P, S], U8, name="cscale%d" % a, align_bytes=64) for a in range(PASSES)]
        scodes = [keep.tile([P, T], U32, name="scodes%d" % a, align_bytes=64) for a in range(PASSES)]
        sscale = [keep.tile([P, T], U8, name="sscale%d" % a, align_bytes=64) for a in range(PASSES)]
        y = keep.tile([P, S], F32, name="y")
        ys = keep.tile([P, T], F32, name="ys")
        g1 = keep.tile([P, T], F32, name="g1")
        g2 = keep.tile([P, T], F32, name="g2")
        ot = keep.tile([P, T], F32, name="ot")

        ps_sa = psum.tile([P, 512], F32, name="ps_sa")
        ps_sb = psum.tile([P, 512], F32, name="ps_sb")
        ps_q = [psum.tile([P, 512], F32, name="ps_q%d" % i) for i in range(2)]
        ps_l = [psum.tile([P, 128], F32, name="ps_l%d" % i) for i in range(4)]

        nc.gpsimd.memset(wsc[:].rearrange("p a n -> p (a n)").bitcast(I32), 0)

        xv = xT.rearrange("(a p j) t -> a p j t", a=PASSES, j=4)
        xr = {}
        H = T // 2

        def load_x(a, u):
            t = xpool.tile([P, 2, T], F32, name="xr")
            if a == 0 and u == 0:
                nc.sync.dma_start(out=t[:, :, :H], in_=xv[a][:, 2 * u:2 * u + 2, :H])
                nc.sync.dma_start(out=t[:, :, H:], in_=xv[a][:, 2 * u:2 * u + 2, H:])
            else:
                nc.sync.dma_start(out=t[:], in_=xv[a][:, 2 * u:2 * u + 2, :])
            xr[a, u] = t

        def late_loads():
            load_x(4, 0)
            load_x(4, 1)
            nc.sync.dma_start(out=bias[:], in_=b)
            wsv = w_scales.bitcast(I32).rearrange("e a q n -> q (e a) n")
            for q in range(4):
                nc.sync.dma_start(out=wsc[32 * q:32 * q + 4].rearrange("p a n -> p (a n)").bitcast(I32).rearrange("p (a n) -> p a n", n=N // 4),
                                  in_=wsv[4 * q:4 * q + 4])
            wv = w_words.bitcast(I32).rearrange("e a p n -> p (e a) n")
            wd = wt[:].rearrange("p a n -> p (a n)").bitcast(I32).rearrange("p (a n) -> p a n", n=N // 2)
            for lo, hi in ((40, 65), (0, 20), (20, 40)):
                nc.sync.dma_start(out=wd[:, lo:hi, :], in_=wv[:, lo:hi, :])
            nc.sync.dma_start(out=gate_t[:], in_=gate.rearrange("g p t -> p g t"))
            nc.sync.dma_start(pos1_t[:], pos1)
            nc.sync.dma_start(pos2_t[:], pos2)

        win, gt, goff, gi, sh = {}, {}, {}, {}, {}

        def cast(a, u):
            if a not in win:
                win[a] = winp.tile([P, 2, 2 * T], BF16, name="win", align_bytes=64)
            d = win[a][:, u, :].rearrange("p (t j) -> p t j", j=2)
            s = xr[a, u][:].rearrange("p j t -> p t j")
            if a == 0 and u == 0:
                nc.vector.tensor_copy(out=d[:, :H, :], in_=s[:, :H, :])
                nc.vector.tensor_copy(out=d[:, H:H + 256, :], in_=s[:, H:H + 256, :])
                nc.scalar.copy(out=d[:, H + 256:, :], in_=s[:, H + 256:, :])
            else:
                nc.scalar.copy(out=d, in_=s)

        def s_cast():
            nc.scalar.copy(out=planes[:], in_=xr[4, 1][:])

        def s_gather(lo):
            g = gsp.tile([P, 2, 256], U32, name="gs")
            gt[4, lo] = g
            v = g[:, 1, :].bitcast(BF16).rearrange("p (s j) -> p s j", j=2)
            for s0 in range(0, 256, C):
                for j in range(2):
                    nc.scalar.activation(v[:, s0:s0 + C, j], planes[:, j, :].indirect(offs_t[:, (lo + s0) // 16:(lo + s0 + C) // 16]), COPY)

        def gather(a, lo, n):
            us = (0,) if (a, lo) in gt else (0, 1)
            if (a, lo) not in gt:
                gt[a, lo] = gp.tile([P, 2, 512], U32, name="g")
            for u in us:
                nc.vector.tensor_copy(gt[a, lo][:, u, :n], win[a][:, u, :].bitcast(U32).indirect(offs_t[:, lo // 16:(lo + n) // 16]))

        def inter(a, lo, n):
            t = gip.tile([P, 2 * 1024], BF16, name="gi", align_bytes=64)
            gi[a, lo] = t
            if (a, lo) in VINTER:
                nc.vector.tensor_copy(out=t[:].bitcast(I32)[:, :2 * n].rearrange("p (s u) -> p s u", u=2),
                                      in_=gt[a, lo][:, :, :n].bitcast(I32).rearrange("p u s -> p s u"))
            else:
                nc.scalar.copy(out=t[:].bitcast(U32)[:, :2 * n].rearrange("p (s u) -> p s u", u=2),
                               in_=gt[a, lo][:, :, :n].rearrange("p u s -> p s u"))

        def quant(a, lo, n):
            nc.vector.quantize_mx(out=codes[a][:, lo:lo + n].bitcast(FP8), scales=cscale[a][:, lo:lo + n], in_=gi[a, lo][:, :4 * n])

        def sh_inter(a):
            t = shp.tile([P, 4 * T], BF16, name="sh", align_bytes=64)
            nc.scalar.copy(out=t[:].bitcast(U32).rearrange("p (s u) -> p s u", u=2),
                           in_=win[a][:].rearrange("p u t -> p (u t)").bitcast(U32).rearrange("p (u s) -> p s u", u=2))
            sh[a] = t

        def sh_quant(a):
            for lo, n in ((0, 512), (512, 256)):
                nc.vector.quantize_mx(out=scodes[a][:, lo:lo + n].bitcast(FP8), scales=sscale[a][:, lo:lo + n],
                                      in_=sh[a][:, 4 * lo:4 * (lo + n)])

        def mm(dst, e, a, cd, cs, cols):
            nc.tensor.matmul_mx(out=dst, lhsT=wt[:, e * PASSES + a, :].bitcast(FP4), lhsT_scale=wsc[:, e * PASSES + a, :],
                                rhs=cd[a][:, cols].bitcast(FP8), rhs_scale=cs[a][:, cols], start=a == 0, stop=a == PASSES - 1)

        def shared_mm(a):
            mm(ps_sa[:], E, a, scodes, sscale, slice(0, 512))
            mm(ps_sb[:], E, a, scodes, sscale, slice(256, 768))

        def quad_mm(i):
            for e in range(4 * i, 4 * i + 4):
                for a in range(PASSES):
                    mm(ps_q[i][:, (e % 4) * C:(e % 4 + 1) * C], e, a, codes, cscale, slice(e * C, (e + 1) * C))

        def quad_out(i):
            for e in range(4 * i, 4 * i + 4):
                nc.scalar.activation(out=y[:, e * C:(e + 1) * C], in_=ps_q[i][:, (e % 4) * C:(e % 4 + 1) * C], func=RELU, bias=bias[:, e:e + 1])
            nc.scalar.activation(out=y[:, 512 * i:512 * i + 512], in_=y[:, 512 * i:512 * i + 512], func=SQUARE)

        def last_mm(es, passes):
            for a in passes:
                for e in es:
                    mm(ps_l[e - 8][:], e, a, codes, cscale, slice(e * C, (e + 1) * C))

        def last_out(e0, vector):
            sq = slice(e0 * C, (e0 + 2) * C)
            for e in (e0, e0 + 1):
                cols = slice(e * C, (e + 1) * C)
                if vector:
                    nc.vector.tensor_scalar(out=y[:, cols], in0=ps_l[e - 8][:], scalar1=bias[:, e:e + 1], scalar2=0.0, op0=ADD, op1=MAX)
                else:
                    nc.scalar.activation(out=y[:, cols], in_=ps_l[e - 8][:], func=RELU, bias=bias[:, e:e + 1])
            if vector:
                nc.vector.tensor_tensor(y[:, sq], y[:, sq], y[:, sq], MULT)
            else:
                nc.scalar.activation(out=y[:, sq], in_=y[:, sq], func=SQUARE)

        pend = []

        def flush(depth):
            while len(pend) > depth:
                pend.pop(0)()

        def shared(a):
            sh_inter(a)
            pend.append(lambda: sh_quant(a))

        nc.sync.dma_start(offs_t[:], offs)
        for a in range(4):
            load_x(a, 0)
            load_x(a, 1)
        cast(0, 0)
        cast(0, 1)
        late_loads()

        L = PASSES - 1
        steps = [(a, lo, 512) for a in range(3) for lo in (0, 512, 1024)]
        for lo, n in ((0, 512), (512, 512), (1024, 256), (1280, 256)):
            steps += [(3, lo, n), (4, lo, n)]
        hooks = {
            (0, 0): lambda: (cast(1, 0), cast(1, 1)),
            (0, 512): lambda: cast(2, 0),
            (0, 1024): lambda: shared(0),
            (1, 0): lambda: (last_mm(range(8, 12), [0]), shared(1), s_cast()),
            (1, 512): lambda: (shared_mm(0), shared_mm(1), s_gather(1024)),
            (1, 1024): lambda: (cast(2, 1), cast(3, 0)),
            (2, 0): lambda: (last_mm(range(8, 12), [1]), cast(4, 1)),
            (2, 512): lambda: cast(4, 0),
            (2, 1024): lambda: (cast(3, 1), shared(2)),
            (3, 0): lambda: (last_mm(range(8, 12), [2]), shared_mm(2)),
            (3, 512): lambda: (quad_mm(0), shared(3), s_gather(1280)),
            (4, 512): lambda: (shared_mm(3), shared(4), quad_out(0)),
            (3, 1024): lambda: (quad_mm(1), shared_mm(4)),
            (4, 1024): lambda: (quad_out(1), last_mm((8, 9), [3])),
            (3, 1280): lambda: last_mm((8, 9), [4]),
            (4, 1280): lambda: (last_out(8, False), last_mm((10, 11), [3])),
        }
        for a, lo, n in steps:
            gather(a, lo, n)
            inter(a, lo, n)
            pend.append(lambda a=a, lo=lo, n=n: quant(a, lo, n))
            flush(1)
            if (a, lo) in hooks:
                hooks[a, lo]()
        flush(0)
        last_mm((10, 11), [4])
        last_out(10, True)

        nc.vector.tensor_scalar(out=ys[:, 512:], in0=ps_sb[:, 256:], scalar1=bias[:, E:E + 1], scalar2=0.0, op0=ADD, op1=MAX)
        nc.vector.tensor_tensor(ys[:, 512:], ys[:, 512:], ys[:, 512:], MULT)
        nc.scalar.activation(out=ys[:, :512], in_=ps_sa[:], func=RELU, bias=bias[:, E:E + 1])
        nc.scalar.activation(out=ys[:, :512], in_=ys[:, :512], func=SQUARE)

        nc.vector.tensor_tensor(g1[:], y[:].indirect(pos1_t[:]), gate_t[:, 0, :], MULT)
        nc.vector.tensor_tensor(g1[:], g1[:], ys[:], ADD)
        for lo, n in ((0, 512), (512, 256)):
            c = slice(lo, lo + n)
            nc.vector.tensor_tensor(g2[:, c], y[:].indirect(pos2_t[:, lo // 16:(lo + n) // 16]), gate_t[:, 1, c], MULT)
            nc.vector.tensor_tensor(ot[:, c], g1[:, c], g2[:, c], ADD)
            nc.sync.dma_start(out=out[:, c], in_=ot[:, c])
